import numpy as np
import ml_dtypes


def mxq(x, axis, fmt="e4m3"):
    dtype, down = {"e4m3": (ml_dtypes.float8_e4m3fn, 7), "e5m2": (ml_dtypes.float8_e5m2, 14)}[fmt]
    v = np.moveaxis(np.asarray(x, np.float32).astype(ml_dtypes.bfloat16).astype(np.float64), axis, -1)
    blocks = v.reshape(v.shape[:-1] + (-1, 32))
    amax = np.abs(blocks).max(-1, keepdims=True)
    byte = np.maximum(np.where(amax > 0, np.frexp(amax)[1] - 1 + 127, 0) - down, 1)
    scale = np.exp2(byte - 127.0)
    codes = (blocks / scale).astype(np.float32).astype(dtype).astype(np.float64)
    return np.moveaxis((codes * scale).reshape(v.shape), -1, axis)


WIDE = False


def mx_kscale(k):
    if not WIDE:
        return np.ones(k)
    levels = np.array([10, -10, 5, -5, 0])
    if k % 512:
        return np.exp2(np.random.permutation(np.resize(levels, k // 32))).repeat(32)
    a = np.empty((k // 512, 16))
    for p in range(k // 512):
        a[p, :8] = np.random.permutation(np.resize(levels, 8))
        for g in range(8):
            far = levels[np.abs(levels - a[p, g]) >= 10]
            a[p, g + 8] = far[np.random.randint(len(far))]
    return np.exp2(a.ravel()).repeat(32)


def f64(x):
    return np.asarray(x).astype(np.float64)


def striped(idx):
    return np.tile(idx.reshape(-1, 16).T, (8, 1)).astype(np.uint16)


def unstriped(offs):
    return offs[:16].T.reshape(-1).astype(np.int64)


E2M1 = np.array([0.0, 0.5, 1.0, 1.5, 2.0, 3.0, 4.0, 6.0, -0.0, -0.5, -1.0, -1.5, -2.0, -3.0, -4.0, -6.0])


def pack_weight(w, fmt):
    k, n = w.shape
    w = f64(np.asarray(w, np.float32).astype(ml_dtypes.bfloat16)).reshape(k // 32, 32, n)
    amax = np.abs(w).max(1)
    if fmt == "e4m3":
        byte = np.frexp(amax)[1] - 1 + 127 - 7
    else:
        mant, ex = np.frexp(amax / 6.0)
        byte = np.where(mant > 0.5, ex, ex - 1) + 127
    byte = np.clip(np.where(amax > 0, byte, 1), 1, 254)
    scaled = (w * np.exp2(127.0 - byte)[:, None, :]).reshape(k, n).astype(np.float32)
    by_word = np.ascontiguousarray(scaled.reshape(k // 512, 128, 4, n).transpose(0, 1, 3, 2))
    if fmt == "e4m3":
        words = by_word.astype(ml_dtypes.float8_e4m3fn).view(np.uint8)
    else:
        c = by_word.astype(ml_dtypes.float4_e2m1fn).view(np.uint8) & 0xF
        words = (c[..., 0::2] | (c[..., 1::2] << 4)).reshape(k // 512, 128, 2 * n)
    return np.ascontiguousarray(words), np.ascontiguousarray(byte.astype(np.uint8).reshape(k // 512, 16, n))


def unpack_weight(words, scales, fmt):
    g, _, n = scales.shape
    words = np.ascontiguousarray(words).reshape(g, 128, n, -1)
    if fmt == "e4m3":
        vals = words.view(ml_dtypes.float8_e4m3fn).astype(np.float64)
    else:
        nib = np.empty((g, 128, n, 4), np.uint8)
        nib[..., 0::2] = words & 0xF
        nib[..., 1::2] = words >> 4
        vals = E2M1[nib]
    vals = vals * np.repeat(np.exp2(scales.astype(np.float64) - 127.0), 8, axis=1)[..., None]
    return vals.transpose(0, 1, 3, 2).reshape(g * 512, n)


def pack_table(v):
    words, scales = pack_weight(v, "e4m3")
    return np.concatenate([words.reshape(words.shape[0], -1), scales.reshape(scales.shape[0], -1)], axis=1)


def unpack_table(tab):
    g, t = tab.shape[0], tab.shape[1] // 528
    return unpack_weight(tab[:, :512 * t].reshape(g, 128, t, 4), tab[:, 512 * t:].reshape(g, 16, t), "e4m3")


G, K, M, T, S = 4, 1024, 1024, 2048, 256


def setup_inputs():
    n = np.random.standard_normal
    s = mx_kscale(K)[:, None]
    p_w4 = pack_weight(n((K, M)) / np.sqrt(K) / s, "e2m1")
    return {
        "tab": pack_table(n((K, T)) * s),
        "w4_words": p_w4[0],
        "w4_scales": p_w4[1],
        "dw": (0.3 * n((K, M)) / np.sqrt(K) / s).astype(np.float32),
        "offs": striped(np.concatenate([np.random.permutation(T)[:S] for _ in range(G)])),
    }


def reference(tab, w4_words, w4_scales, dw, offs):
    tab_ = unpack_table(tab)[:, unstriped(offs).reshape(G, S)].sum(1)
    w4_ = unpack_weight(w4_words, w4_scales, "e2m1")
    dw_ = mxq(f64(dw), 0, "e4m3")
    y = w4_.T @ tab_ + dw_.T @ tab_
    return y

@@ -1,0 +1,138 @@
+from contextlib import ExitStack
+
+import concourse.mybir as mybir
+
+G, K, M, T, S = 4, 1024, 1024, 2048, 256
+FLOPS = 2 * 2 * G * K * M * S
+
+F32 = mybir.dt.float32
+BF16 = mybir.dt.bfloat16
+I32 = mybir.dt.int32
+U32 = mybir.dt.uint32
+U16 = mybir.dt.uint16
+U8 = mybir.dt.uint8
+FP8X4 = mybir.dt.float8_e4m3fn_x4
+FP4X4 = mybir.dt.float4_e2m1fn_x4
+
+P = 128
+PACK = 4
+K_PASS = P * PACK
+PASSES = K // K_PASS
+QUADS = 4
+N_TILES = M // P
+HALF = 512
+WORD_BYTES = K_PASS * T
+LIST_COLS = S // 16
+
+
+def tile_list_tabbag_sum_none_kernel(tc, tab, w4_words, w4_scales, dw, offs, out):
+    nc = tc.nc
+    with ExitStack() as ctx:
+        keep = ctx.enter_context(tc.tile_pool(name="keep", bufs=1))
+        stage = ctx.enter_context(tc.tile_pool(name="stage", bufs=3))
+        psum = ctx.enter_context(tc.psum_pool(name="psum", bufs=1))
+
+        offsets = keep.tile([P, G * LIST_COLS], U16, name="offsets")
+        tab_words = [keep.tile([P, T], I32, name=f"tab_words{a}", align_bytes=64) for a in range(PASSES)]
+        tab_scales = [keep.tile([P, T], U8, name=f"tab_scales{a}", align_bytes=64) for a in range(PASSES)]
+        w4_codes = [keep.tile([P, 2 * M], U8, name=f"w4_codes{a}", align_bytes=64) for a in range(PASSES)]
+        w4_plane = keep.tile([P, PASSES, M], U8, name="w4_plane", align_bytes=64)
+        bag_words = [[keep.tile([P, S], U32, name=f"bag_words{a}_{g}", align_bytes=64) for g in range(G)] for a in range(PASSES)]
+        bag_scales = [[keep.tile([P, S], U8, name=f"bag_scales{a}_{g}", align_bytes=64) for g in range(G)] for a in range(PASSES)]
+        dw_raw = {}
+        dw_codes = {}
+        dw_scales = {}
+        for h in range(M // HALF):
+            for a in range(PASSES):
+                dw_raw[a, h] = keep.tile([P, PACK, HALF], F32, name=f"dw_raw{a}_{h}")
+        for n in range(N_TILES):
+            for a in range(PASSES):
+                dw_codes[a, n] = keep.tile([P, P], U32, name=f"dw_codes{a}_{n}", align_bytes=64)
+                dw_scales[a, n] = keep.tile([P, P], U8, name=f"dw_scales{a}_{n}", align_bytes=64)
+        banks = [psum.tile([P, S], F32, name=f"bank{n}") for n in range(N_TILES)]
+
+        def load_tab_words(a):
+            nc.sync.dma_start(tab_words[a][:], tab[a, 0:WORD_BYTES].rearrange("(p b) -> p b", p=P).bitcast(I32))
+
+        def load_tab_scales(a):
+            rows = tab[a, WORD_BYTES:].rearrange("(q t) -> q t", q=16)
+            for q in range(QUADS):
+                nc.scalar.dma_start(tab_scales[a][32 * q : 32 * q + 4, :].bitcast(I32), rows[4 * q : 4 * q + 4, :].bitcast(I32))
+
+        def load_w4_codes(a):
+            nc.sync.dma_start(w4_codes[a][:].bitcast(I32), w4_words[a].bitcast(I32))
+
+        def gather(a, g):
+            picked = offsets[:, g * LIST_COLS : (g + 1) * LIST_COLS]
+            nc.vector.tensor_copy(bag_scales[a][g][:], tab_scales[a][:].indirect(picked))
+            nc.vector.tensor_copy(bag_words[a][g][:], tab_words[a][:].bitcast(U32).indirect(picked))
+
+        nc.vector.memset(tab_scales[0][:].bitcast(I32), 0)
+        nc.vector.memset(w4_plane[:].rearrange("p a n -> p (a n)").bitcast(I32), 0)
+        nc.vector.memset(tab_scales[1][:].bitcast(I32), 0)
+
+        nc.sync.dma_start(offsets[:], offs)
+        load_tab_words(0)
+        load_tab_scales(0)
+        load_w4_codes(0)
+        for q in range(QUADS):
+            nc.scalar.dma_start(
+                w4_plane[32 * q : 32 * q + 4, :, :].bitcast(I32),
+                w4_scales[:, 4 * q : 4 * q + 4, :].rearrange("a r n -> r a n").bitcast(I32),
+            )
+        load_tab_words(1)
+        load_tab_scales(1)
+        load_w4_codes(1)
+        for h in range(M // HALF):
+            for a in range(PASSES):
+                rows = dw[a * K_PASS : (a + 1) * K_PASS, h * HALF : (h + 1) * HALF]
+                nc.sync.dma_start(dw_raw[a, h][:], rows.rearrange("(p j) n -> p j n", j=PACK))
+
+        for a in range(PASSES):
+            for g in range(G):
+                gather(a, g)
+
+        for a in range(PASSES):
+            for g in range(G):
+                for n in range(N_TILES):
+                    for c in range(S // P):
+                        cols = slice(c * P, (c + 1) * P)
+                        nc.tensor.matmul_mx(
+                            out=banks[n][:, cols],
+                            lhsT=w4_codes[a][:, 2 * P * n : 2 * P * (n + 1)].bitcast(FP4X4),
+                            lhsT_scale=w4_plane[:, a, P * n : P * (n + 1)],
+                            rhs=bag_words[a][g][:, cols].bitcast(FP8X4),
+                            rhs_scale=bag_scales[a][g][:, cols],
+                            start=(a == 0 and g == 0 and c == 0),
+                            stop=False,
+                        )
+
+        for n in range(N_TILES):
+            h, c0 = divmod(n * P, HALF)
+            for a in range(PASSES):
+                grouped = stage.tile([P, P, PACK], BF16, name="grouped", align_bytes=64)
+                nc.scalar.copy(
+                    grouped[:].rearrange("p (c i) t -> p c t i", i=4),
+                    dw_raw[a, h][:, :, c0 : c0 + P].rearrange("p t (c i) -> p c t i", i=4),
+                )
+                nc.vector.quantize_mx(
+                    out=dw_codes[a, n][:].bitcast(FP8X4),
+                    scales=dw_scales[a, n][:],
+                    in_=grouped[:].rearrange("p c t -> p (c t)"),
+                )
+
+        for n in range(N_TILES):
+            for a in range(PASSES):
+                for g in range(G):
+                    nc.tensor.matmul_mx(
+                        out=banks[n][:],
+                        lhsT=dw_codes[a, n][:].bitcast(FP8X4),
+                        lhsT_scale=dw_scales[a, n][:],
+                        rhs=bag_words[a][g][:].bitcast(FP8X4),
+                        rhs_scale=bag_scales[a][g][:],
+                        start=False,
+                        stop=(a == PASSES - 1 and g == G - 1),
+                    )
+            result = stage.tile([P, S], F32, name="result")
+            nc.vector.tensor_copy(result[:], banks[n][:])
+            nc.sync.dma_start(out[n * P : (n + 1) * P, :], result[:])

@@ -23,28 +23,48 @@ N_TILES = M // P
 HALF = 512
 WORD_BYTES = K_PASS * T
 LIST_COLS = S // 16
+KIB = 1024
+ZERO_SPLIT = 320
 
 
 def tile_list_tabbag_sum_none_kernel(tc, tab, w4_words, w4_scales, dw, offs, out):
     nc = tc.nc
     with ExitStack() as ctx:
         keep = ctx.enter_context(tc.tile_pool(name="keep", bufs=1))
-        stage = ctx.enter_context(tc.tile_pool(name="stage", bufs=3))
+        relay = ctx.enter_context(tc.tile_pool(name="relay", bufs=1))
+        stage = ctx.enter_context(tc.tile_pool(name="stage", bufs=4))
         psum = ctx.enter_context(tc.psum_pool(name="psum", bufs=1))
 
         offsets = keep.tile([P, G * LIST_COLS], U16, name="offsets")
-        tab_words = [keep.tile([P, T], I32, name=f"tab_words{a}", align_bytes=64) for a in range(PASSES)]
-        tab_scales = [keep.tile([P, T], U8, name=f"tab_scales{a}", align_bytes=64) for a in range(PASSES)]
-        w4_codes = [keep.tile([P, 2 * M], U8, name=f"w4_codes{a}", align_bytes=64) for a in range(PASSES)]
-        w4_plane = keep.tile([P, PASSES, M], U8, name="w4_plane", align_bytes=64)
+        tab_words = [
+            relay.tile([P, T], I32, name="tab_words0", offset=20 * KIB, align_bytes=64),
+            relay.tile([P, T], I32, name="tab_words1", offset=0, align_bytes=64),
+        ]
+        tab_scales = [
+            relay.tile([P, T], U8, name="tab_scales0", offset=47 * KIB + 512, align_bytes=64),
+            keep.tile([P, T], U8, name="tab_scales1", align_bytes=64),
+        ]
+        w4_codes = [
+            relay.tile([P, 2 * M], U8, name="w4_codes0", offset=60 * KIB, align_bytes=64),
+            relay.tile([P, 2 * M], U8, name="w4_codes1", offset=8 * KIB, align_bytes=64),
+        ]
+        w4_planes = [keep.tile([P, M], U8, name=f"w4_plane{a}", align_bytes=64) for a in range(PASSES)]
         bag_words = [[keep.tile([P, S], U32, name=f"bag_words{a}_{g}", align_bytes=64) for g in range(G)] for a in range(PASSES)]
-        bag_scales = [[keep.tile([P, S], U8, name=f"bag_scales{a}_{g}", align_bytes=64) for g in range(G)] for a in range(PASSES)]
+        first_pick = relay.tile([P, 2 * S], U8, name="first_pick", offset=8 * KIB - S, align_bytes=64)
+        pair_scales = {
+            (0, 0): keep.tile([P, 2 * S], U8, name="scales0_low", align_bytes=64),
+            (0, 1): relay.tile([P, 2 * S], U8, name="scales0_high", offset=24 * KIB, align_bytes=64),
+            (1, 0): relay.tile([P, 2 * S], U8, name="scales1_low", offset=48 * KIB, align_bytes=64),
+            (1, 1): relay.tile([P, 2 * S], U8, name="scales1_high", offset=60 * KIB, align_bytes=64),
+        }
+        bag_scales = [[pair_scales[a, g // 2][:, (g % 2) * S : (g % 2 + 1) * S] for g in range(G)] for a in range(PASSES)]
+        raw_offsets = {(0, 0): 16 * KIB, (1, 0): 25 * KIB, (0, 1): 40 * KIB, (1, 1): 49 * KIB}
         dw_raw = {}
         dw_codes = {}
         dw_scales = {}
         for h in range(M // HALF):
             for a in range(PASSES):
-                dw_raw[a, h] = keep.tile([P, PACK, HALF], F32, name=f"dw_raw{a}_{h}")
+                dw_raw[a, h] = relay.tile([P, PACK, HALF], F32, name=f"dw_raw{a}_{h}", offset=raw_offsets[a, h], align_bytes=64)
         for n in range(N_TILES):
             for a in range(PASSES):
                 dw_codes[a, n] = keep.tile([P, P], U32, name=f"dw_codes{a}_{n}", align_bytes=64)
@@ -54,45 +74,31 @@ def tile_list_tabbag_sum_none_kernel(tc, tab, w4_words, w4_scales, dw, offs, out
         def load_tab_words(a):
             nc.sync.dma_start(tab_words[a][:], tab[a, 0:WORD_BYTES].rearrange("(p b) -> p b", p=P).bitcast(I32))
 
-        def load_tab_scales(a):
+        def load_tab_scales(a, queues):
             rows = tab[a, WORD_BYTES:].rearrange("(q t) -> q t", q=16)
             for q in range(QUADS):
-                nc.scalar.dma_start(tab_scales[a][32 * q : 32 * q + 4, :].bitcast(I32), rows[4 * q : 4 * q + 4, :].bitcast(I32))
+                queues[q % len(queues)].dma_start(tab_scales[a][q:P:32, :].bitcast(I32), rows[q:16:4, :].bitcast(I32))
 
-        def load_w4_codes(a):
-            nc.sync.dma_start(w4_codes[a][:].bitcast(I32), w4_words[a].bitcast(I32))
+        def load_w4_codes(a, lo, hi):
+            nc.sync.dma_start(w4_codes[a][:, lo:hi].bitcast(I32), w4_words[a][:, lo:hi].bitcast(I32))
 
-        def gather(a, g):
+        def load_w4_scales(a):
+            for q in range(QUADS):
+                nc.sync.dma_start(w4_planes[a][q:P:32, :].bitcast(I32), w4_scales[a][q:16:4, :].bitcast(I32))
+
+        def load_dw(a, h):
+            rows = dw[a * K_PASS : (a + 1) * K_PASS, h * HALF : (h + 1) * HALF]
+            nc.sync.dma_start(dw_raw[a, h][:], rows.rearrange("(p j) n -> p j n", j=PACK))
+
+        def gather_scales(into, a, g0, g1):
+            picked = offsets[:, g0 * LIST_COLS : g1 * LIST_COLS]
+            nc.vector.tensor_copy(into, tab_scales[a][:].indirect(picked))
+
+        def gather_words(a, g):
             picked = offsets[:, g * LIST_COLS : (g + 1) * LIST_COLS]
-            nc.vector.tensor_copy(bag_scales[a][g][:], tab_scales[a][:].indirect(picked))
             nc.vector.tensor_copy(bag_words[a][g][:], tab_words[a][:].bitcast(U32).indirect(picked))
 
-        nc.vector.memset(tab_scales[0][:].bitcast(I32), 0)
-        nc.vector.memset(w4_plane[:].rearrange("p a n -> p (a n)").bitcast(I32), 0)
-        nc.vector.memset(tab_scales[1][:].bitcast(I32), 0)
-
-        nc.sync.dma_start(offsets[:], offs)
-        load_tab_words(0)
-        load_tab_scales(0)
-        load_w4_codes(0)
-        for q in range(QUADS):
-            nc.scalar.dma_start(
-                w4_plane[32 * q : 32 * q + 4, :, :].bitcast(I32),
-                w4_scales[:, 4 * q : 4 * q + 4, :].rearrange("a r n -> r a n").bitcast(I32),
-            )
-        load_tab_words(1)
-        load_tab_scales(1)
-        load_w4_codes(1)
-        for h in range(M // HALF):
-            for a in range(PASSES):
-                rows = dw[a * K_PASS : (a + 1) * K_PASS, h * HALF : (h + 1) * HALF]
-                nc.sync.dma_start(dw_raw[a, h][:], rows.rearrange("(p j) n -> p j n", j=PACK))
-
-        for a in range(PASSES):
-            for g in range(G):
-                gather(a, g)
-
-        for a in range(PASSES):
+        def multiply_w4(a):
             for g in range(G):
                 for n in range(N_TILES):
                     for c in range(S // P):
@@ -100,18 +106,53 @@ def tile_list_tabbag_sum_none_kernel(tc, tab, w4_words, w4_scales, dw, offs, out
                         nc.tensor.matmul_mx(
                             out=banks[n][:, cols],
                             lhsT=w4_codes[a][:, 2 * P * n : 2 * P * (n + 1)].bitcast(FP4X4),
-                            lhsT_scale=w4_plane[:, a, P * n : P * (n + 1)],
+                            lhsT_scale=w4_planes[a][:, P * n : P * (n + 1)],
                             rhs=bag_words[a][g][:, cols].bitcast(FP8X4),
                             rhs_scale=bag_scales[a][g][:, cols],
                             start=(a == 0 and g == 0 and c == 0),
                             stop=False,
                         )
 
+        first_plane = tab_scales[0][:].bitcast(I32)
+        nc.vector.memset(first_plane[:, 0:ZERO_SPLIT], 0)
+        nc.gpsimd.memset(first_plane[:, ZERO_SPLIT:], 0)
+        nc.vector.memset(w4_planes[0][:].bitcast(I32), 0)
+        nc.vector.memset(tab_scales[1][:].bitcast(I32), 0)
+        nc.vector.memset(w4_planes[1][:].bitcast(I32), 0)
+
+        nc.sync.dma_start(offsets[:], offs)
+        load_w4_codes(0, 0, M)
+        load_w4_codes(0, M, 2 * M)
+        load_tab_scales(0, [nc.scalar, nc.sync])
+        load_tab_words(0)
+        load_w4_scales(0)
+        load_tab_scales(1, [nc.sync])
+        load_w4_scales(1)
+
+        gather_scales(first_pick[:], 0, 0, 2)
+        nc.vector.tensor_copy(pair_scales[0, 0][:].bitcast(I32), first_pick[:].bitcast(I32))
+        load_tab_words(1)
+        load_w4_codes(1, 0, 2 * M)
+        for g in range(G):
+            gather_words(0, g)
+        load_dw(0, 0)
+        load_dw(1, 0)
+        gather_scales(pair_scales[0, 1][:], 0, 2, 4)
+        load_dw(0, 1)
+        load_dw(1, 1)
+        multiply_w4(0)
+        for g in range(G):
+            if g % 2 == 0:
+                gather_scales(pair_scales[1, g // 2][:], 1, g, g + 2)
+            gather_words(1, g)
+        multiply_w4(1)
+
         for n in range(N_TILES):
             h, c0 = divmod(n * P, HALF)
             for a in range(PASSES):
-                grouped = stage.tile([P, P, PACK], BF16, name="grouped", align_bytes=64)
-                nc.scalar.copy(
+                grouped = stage.tile([P, P, PACK], BF16, name=f"grouped{a}", align_bytes=64)
+                interleave = nc.scalar.copy if a == 0 else nc.vector.tensor_copy
+                interleave(
                     grouped[:].rearrange("p (c i) t -> p c t i", i=4),
                     dw_raw[a, h][:, :, c0 : c0 + P].rearrange("p t (c i) -> p c t i", i=4),
                 )
@@ -129,10 +170,11 @@ def tile_list_tabbag_sum_none_kernel(tc, tab, w4_words, w4_scales, dw, offs, out
                         lhsT=dw_codes[a, n][:].bitcast(FP8X4),
                         lhsT_scale=dw_scales[a, n][:],
                         rhs=bag_words[a][g][:].bitcast(FP8X4),
-                        rhs_scale=bag_scales[a][g][:],
+                        rhs_scale=bag_scales[a][g],
                         start=False,
                         stop=(a == PASSES - 1 and g == G - 1),
                     )
             result = stage.tile([P, S], F32, name="result")
-            nc.vector.tensor_copy(result[:], banks[n][:])
+            empty = nc.scalar.copy if n % 2 == 0 else nc.vector.tensor_copy
+            empty(result[:], banks[n][:])
             nc.sync.dma_start(out[n * P : (n + 1) * P, :], result[:])

@@ -24,6 +24,10 @@ HALF = 512
 WORD_BYTES = K_PASS * T
 LIST_COLS = S // 16
 KIB = 1024
+LEAD = 512
+EARLY = G - 1
+WARM_COLS = 32
+WARM_PASSES = 20
 ZERO_SPLIT = 320
 
 
@@ -45,19 +49,20 @@ def tile_list_tabbag_sum_none_kernel(tc, tab, w4_words, w4_scales, dw, offs, out
             keep.tile([P, T], U8, name="tab_scales1", align_bytes=64),
         ]
         w4_codes = [
-            relay.tile([P, 2 * M], U8, name="w4_codes0", offset=60 * KIB, align_bytes=64),
+            keep.tile([P, 2 * M], U8, name="w4_codes0", align_bytes=64),
             relay.tile([P, 2 * M], U8, name="w4_codes1", offset=8 * KIB, align_bytes=64),
         ]
         w4_planes = [keep.tile([P, M], U8, name=f"w4_plane{a}", align_bytes=64) for a in range(PASSES)]
         bag_words = [[keep.tile([P, S], U32, name=f"bag_words{a}_{g}", align_bytes=64) for g in range(G)] for a in range(PASSES)]
-        first_pick = relay.tile([P, 2 * S], U8, name="first_pick", offset=8 * KIB - S, align_bytes=64)
-        pair_scales = {
-            (0, 0): keep.tile([P, 2 * S], U8, name="scales0_low", align_bytes=64),
-            (0, 1): relay.tile([P, 2 * S], U8, name="scales0_high", offset=24 * KIB, align_bytes=64),
-            (1, 0): relay.tile([P, 2 * S], U8, name="scales1_low", offset=48 * KIB, align_bytes=64),
-            (1, 1): relay.tile([P, 2 * S], U8, name="scales1_high", offset=60 * KIB, align_bytes=64),
-        }
-        bag_scales = [[pair_scales[a, g // 2][:, (g % 2) * S : (g % 2 + 1) * S] for g in range(G)] for a in range(PASSES)]
+        early_scales = [
+            keep.tile([P, EARLY * S], U8, name="early_scales0", align_bytes=64),
+            relay.tile([P, EARLY * S], U8, name="early_scales1", offset=24 * KIB + S, align_bytes=64),
+        ]
+        last_scales = [
+            relay.tile([P, S], U8, name="last_scales0", offset=24 * KIB, align_bytes=64),
+            relay.tile([P, S], U8, name="last_scales1", offset=0, align_bytes=64),
+        ]
+        bag_scales = [[early_scales[a][:, g * S : (g + 1) * S] for g in range(EARLY)] + [last_scales[a][:]] for a in range(PASSES)]
         raw_offsets = {(0, 0): 16 * KIB, (1, 0): 25 * KIB, (0, 1): 40 * KIB, (1, 1): 49 * KIB}
         dw_raw = {}
         dw_codes = {}
@@ -71,8 +76,9 @@ def tile_list_tabbag_sum_none_kernel(tc, tab, w4_words, w4_scales, dw, offs, out
                 dw_scales[a, n] = keep.tile([P, P], U8, name=f"dw_scales{a}_{n}", align_bytes=64)
         banks = [psum.tile([P, S], F32, name=f"bank{n}") for n in range(N_TILES)]
 
-        def load_tab_words(a):
-            nc.sync.dma_start(tab_words[a][:], tab[a, 0:WORD_BYTES].rearrange("(p b) -> p b", p=P).bitcast(I32))
+        def load_tab_words(a, lo, hi):
+            words = tab[a, 0:WORD_BYTES].rearrange("(p b) -> p b", p=P).bitcast(I32)
+            nc.sync.dma_start(tab_words[a][:, lo:hi], words[:, lo:hi])
 
         def load_tab_scales(a, queues):
             rows = tab[a, WORD_BYTES:].rearrange("(q t) -> q t", q=16)
@@ -116,35 +122,59 @@ def tile_list_tabbag_sum_none_kernel(tc, tab, w4_words, w4_scales, dw, offs, out
         first_plane = tab_scales[0][:].bitcast(I32)
         nc.vector.memset(first_plane[:, 0:ZERO_SPLIT], 0)
         nc.gpsimd.memset(first_plane[:, ZERO_SPLIT:], 0)
+        warm_raw = keep.tile([P, PACK, WARM_COLS], F32, name="warm_raw")
+        warm_grouped = keep.tile([P, WARM_COLS, PACK], BF16, name="warm_grouped", align_bytes=64)
+        warm_codes = relay.tile([P, P], U32, name="warm_codes", offset=8 * KIB - 256, align_bytes=64)
+        warm_scales = keep.tile([P, P], U8, name="warm_scales", align_bytes=64)
+        nc.gpsimd.memset(warm_codes[:], 0)
+        nc.gpsimd.memset(warm_scales[:].bitcast(I32), 0)
         nc.vector.memset(w4_planes[0][:].bitcast(I32), 0)
         nc.vector.memset(tab_scales[1][:].bitcast(I32), 0)
         nc.vector.memset(w4_planes[1][:].bitcast(I32), 0)
 
         nc.sync.dma_start(offsets[:], offs)
-        load_w4_codes(0, 0, M)
-        load_w4_codes(0, M, 2 * M)
+        nc.sync.dma_start(warm_raw[:], dw[0:K_PASS, 0:WARM_COLS].rearrange("(p j) n -> p j n", j=PACK))
+        load_tab_words(0, 0, LEAD)
         load_tab_scales(0, [nc.scalar, nc.sync])
-        load_tab_words(0)
+        load_tab_words(0, LEAD, T)
+        load_w4_codes(0, 0, M)
         load_w4_scales(0)
+        load_w4_codes(0, M, 2 * M)
         load_tab_scales(1, [nc.sync])
         load_w4_scales(1)
 
-        gather_scales(first_pick[:], 0, 0, 2)
-        nc.vector.tensor_copy(pair_scales[0, 0][:].bitcast(I32), first_pick[:].bitcast(I32))
-        load_tab_words(1)
+        nc.vector.tensor_copy(warm_grouped[:], warm_raw[:].rearrange("p t c -> p c t"))
+        nc.vector.quantize_mx(
+            out=warm_codes[:, 0:WARM_COLS].bitcast(FP8X4),
+            scales=warm_scales[:, 0:WARM_COLS],
+            in_=warm_grouped[:].rearrange("p c t -> p (c t)"),
+        )
+        for i in range(WARM_PASSES):
+            nc.tensor.matmul_mx(
+                out=banks[N_TILES - 1][:, 0:P],
+                lhsT=warm_codes[:].bitcast(FP8X4),
+                lhsT_scale=warm_scales[:],
+                rhs=warm_codes[:].bitcast(FP8X4),
+                rhs_scale=warm_scales[:],
+                start=True,
+                stop=True,
+            )
+
+        gather_scales(early_scales[0][:], 0, 0, EARLY)
+        load_tab_words(1, 0, T)
         load_w4_codes(1, 0, 2 * M)
         for g in range(G):
             gather_words(0, g)
         load_dw(0, 0)
         load_dw(1, 0)
-        gather_scales(pair_scales[0, 1][:], 0, 2, 4)
+        gather_scales(last_scales[0][:], 0, EARLY, G)
         load_dw(0, 1)
         load_dw(1, 1)
         multiply_w4(0)
+        gather_scales(early_scales[1][:], 1, 0, EARLY)
         for g in range(G):
-            if g % 2 == 0:
-                gather_scales(pair_scales[1, g // 2][:], 1, g, g + 2)
             gather_words(1, g)
+        gather_scales(last_scales[1][:], 1, EARLY, G)
         multiply_w4(1)
 
         for n in range(N_TILES):
@@ -175,6 +205,6 @@ def tile_list_tabbag_sum_none_kernel(tc, tab, w4_words, w4_scales, dw, offs, out
                         stop=(a == PASSES - 1 and g == G - 1),
                     )
             result = stage.tile([P, S], F32, name="result")
-            empty = nc.scalar.copy if n % 2 == 0 else nc.vector.tensor_copy
+            empty = nc.scalar.copy if n < N_TILES - 1 else nc.vector.tensor_copy
             empty(result[:], banks[n][:])
             nc.sync.dma_start(out[n * P : (n + 1) * P, :], result[:])

from contextlib import ExitStack

import concourse.mybir as mybir

G, K, M, T, S = 4, 1024, 1024, 2048, 256
FLOPS = 2 * 2 * G * K * M * S

F32 = mybir.dt.float32
BF16 = mybir.dt.bfloat16
I32 = mybir.dt.int32
U32 = mybir.dt.uint32
U16 = mybir.dt.uint16
U8 = mybir.dt.uint8
FP8X4 = mybir.dt.float8_e4m3fn_x4
FP4X4 = mybir.dt.float4_e2m1fn_x4

P = 128
PACK = 4
K_PASS = P * PACK
PASSES = K // K_PASS
QUADS = 4
N_TILES = M // P
HALF = 512
WORD_BYTES = K_PASS * T
LIST_COLS = S // 16
KIB = 1024
LEAD = 512
EARLY = G - 1
WARM_COLS = 32
WARM_PASSES = 20
ZERO_SPLIT = 320


def tile_list_tabbag_sum_none_kernel(tc, tab, w4_words, w4_scales, dw, offs, out):
    nc = tc.nc
    with ExitStack() as ctx:
        keep = ctx.enter_context(tc.tile_pool(name="keep", bufs=1))
        relay = ctx.enter_context(tc.tile_pool(name="relay", bufs=1))
        stage = ctx.enter_context(tc.tile_pool(name="stage", bufs=4))
        psum = ctx.enter_context(tc.psum_pool(name="psum", bufs=1))

        offsets = keep.tile([P, G * LIST_COLS], U16, name="offsets")
        tab_words = [
            relay.tile([P, T], I32, name="tab_words0", offset=20 * KIB, align_bytes=64),
            relay.tile([P, T], I32, name="tab_words1", offset=0, align_bytes=64),
        ]
        tab_scales = [
            relay.tile([P, T], U8, name="tab_scales0", offset=47 * KIB + 512, align_bytes=64),
            keep.tile([P, T], U8, name="tab_scales1", align_bytes=64),
        ]
        w4_codes = [
            keep.tile([P, 2 * M], U8, name="w4_codes0", align_bytes=64),
            relay.tile([P, 2 * M], U8, name="w4_codes1", offset=8 * KIB, align_bytes=64),
        ]
        w4_planes = [keep.tile([P, M], U8, name=f"w4_plane{a}", align_bytes=64) for a in range(PASSES)]
        bag_words = [[keep.tile([P, S], U32, name=f"bag_words{a}_{g}", align_bytes=64) for g in range(G)] for a in range(PASSES)]
        early_scales = [
            keep.tile([P, EARLY * S], U8, name="early_scales0", align_bytes=64),
            relay.tile([P, EARLY * S], U8, name="early_scales1", offset=24 * KIB + S, align_bytes=64),
        ]
        last_scales = [
            relay.tile([P, S], U8, name="last_scales0", offset=24 * KIB, align_bytes=64),
            relay.tile([P, S], U8, name="last_scales1", offset=0, align_bytes=64),
        ]
        bag_scales = [[early_scales[a][:, g * S : (g + 1) * S] for g in range(EARLY)] + [last_scales[a][:]] for a in range(PASSES)]
        raw_offsets = {(0, 0): 16 * KIB, (1, 0): 25 * KIB, (0, 1): 40 * KIB, (1, 1): 49 * KIB}
        dw_raw = {}
        dw_codes = {}
        dw_scales = {}
        for h in range(M // HALF):
            for a in range(PASSES):
                dw_raw[a, h] = relay.tile([P, PACK, HALF], F32, name=f"dw_raw{a}_{h}", offset=raw_offsets[a, h], align_bytes=64)
        for n in range(N_TILES):
            for a in range(PASSES):
                dw_codes[a, n] = keep.tile([P, P], U32, name=f"dw_codes{a}_{n}", align_bytes=64)
                dw_scales[a, n] = keep.tile([P, P], U8, name=f"dw_scales{a}_{n}", align_bytes=64)
        banks = [psum.tile([P, S], F32, name=f"bank{n}") for n in range(N_TILES)]

        def load_tab_words(a, lo, hi):
            words = tab[a, 0:WORD_BYTES].rearrange("(p b) -> p b", p=P).bitcast(I32)
            nc.sync.dma_start(tab_words[a][:, lo:hi], words[:, lo:hi])

        def load_tab_scales(a, queues):
            rows = tab[a, WORD_BYTES:].rearrange("(q t) -> q t", q=16)
            for q in range(QUADS):
                queues[q % len(queues)].dma_start(tab_scales[a][q:P:32, :].bitcast(I32), rows[q:16:4, :].bitcast(I32))

        def load_w4_codes(a, lo, hi):
            nc.sync.dma_start(w4_codes[a][:, lo:hi].bitcast(I32), w4_words[a][:, lo:hi].bitcast(I32))

        def load_w4_scales(a):
            for q in range(QUADS):
                nc.sync.dma_start(w4_planes[a][q:P:32, :].bitcast(I32), w4_scales[a][q:16:4, :].bitcast(I32))

        def load_dw(a, h):
            rows = dw[a * K_PASS : (a + 1) * K_PASS, h * HALF : (h + 1) * HALF]
            nc.sync.dma_start(dw_raw[a, h][:], rows.rearrange("(p j) n -> p j n", j=PACK))

        def gather_scales(into, a, g0, g1):
            picked = offsets[:, g0 * LIST_COLS : g1 * LIST_COLS]
            nc.vector.tensor_copy(into, tab_scales[a][:].indirect(picked))

        def gather_words(a, g):
            picked = offsets[:, g * LIST_COLS : (g + 1) * LIST_COLS]
            nc.vector.tensor_copy(bag_words[a][g][:], tab_words[a][:].bitcast(U32).indirect(picked))

        def multiply_w4(a):
            for g in range(G):
                for n in range(N_TILES):
                    for c in range(S // P):
                        cols = slice(c * P, (c + 1) * P)
                        nc.tensor.matmul_mx(
                            out=banks[n][:, cols],
                            lhsT=w4_codes[a][:, 2 * P * n : 2 * P * (n + 1)].bitcast(FP4X4),
                            lhsT_scale=w4_planes[a][:, P * n : P * (n + 1)],
                            rhs=bag_words[a][g][:, cols].bitcast(FP8X4),
                            rhs_scale=bag_scales[a][g][:, cols],
                            start=(a == 0 and g == 0 and c == 0),
                            stop=False,
                        )

        first_plane = tab_scales[0][:].bitcast(I32)
        nc.vector.memset(first_plane[:, 0:ZERO_SPLIT], 0)
        nc.gpsimd.memset(first_plane[:, ZERO_SPLIT:], 0)
        warm_raw = keep.tile([P, PACK, WARM_COLS], F32, name="warm_raw")
        warm_grouped = keep.tile([P, WARM_COLS, PACK], BF16, name="warm_grouped", align_bytes=64)
        warm_codes = relay.tile([P, P], U32, name="warm_codes", offset=8 * KIB - 256, align_bytes=64)
        warm_scales = keep.tile([P, P], U8, name="warm_scales", align_bytes=64)
        nc.gpsimd.memset(warm_codes[:], 0)
        nc.gpsimd.memset(warm_scales[:].bitcast(I32), 0)
        nc.vector.memset(w4_planes[0][:].bitcast(I32), 0)
        nc.vector.memset(tab_scales[1][:].bitcast(I32), 0)
        nc.vector.memset(w4_planes[1][:].bitcast(I32), 0)

        nc.sync.dma_start(offsets[:], offs)
        nc.sync.dma_start(warm_raw[:], dw[0:K_PASS, 0:WARM_COLS].rearrange("(p j) n -> p j n", j=PACK))
        load_tab_words(0, 0, LEAD)
        load_tab_scales(0, [nc.scalar, nc.sync])
        load_tab_words(0, LEAD, T)
        load_w4_codes(0, 0, M)
        load_w4_scales(0)
        load_w4_codes(0, M, 2 * M)
        load_tab_scales(1, [nc.sync])
        load_w4_scales(1)

        nc.vector.tensor_copy(warm_grouped[:], warm_raw[:].rearrange("p t c -> p c t"))
        nc.vector.quantize_mx(
            out=warm_codes[:, 0:WARM_COLS].bitcast(FP8X4),
            scales=warm_scales[:, 0:WARM_COLS],
            in_=warm_grouped[:].rearrange("p c t -> p (c t)"),
        )
        for i in range(WARM_PASSES):
            nc.tensor.matmul_mx(
                out=banks[N_TILES - 1][:, 0:P],
                lhsT=warm_codes[:].bitcast(FP8X4),
                lhsT_scale=warm_scales[:],
                rhs=warm_codes[:].bitcast(FP8X4),
                rhs_scale=warm_scales[:],
                start=True,
                stop=True,
            )

        gather_scales(early_scales[0][:], 0, 0, EARLY)
        load_tab_words(1, 0, T)
        load_w4_codes(1, 0, 2 * M)
        for g in range(G):
            gather_words(0, g)
        load_dw(0, 0)
        load_dw(1, 0)
        gather_scales(last_scales[0][:], 0, EARLY, G)
        load_dw(0, 1)
        load_dw(1, 1)
        multiply_w4(0)
        gather_scales(early_scales[1][:], 1, 0, EARLY)
        for g in range(G):
            gather_words(1, g)
        gather_scales(last_scales[1][:], 1, EARLY, G)
        multiply_w4(1)

        for n in range(N_TILES):
            h, c0 = divmod(n * P, HALF)
            for a in range(PASSES):
                grouped = stage.tile([P, P, PACK], BF16, name=f"grouped{a}", align_bytes=64)
                interleave = nc.scalar.copy if a == 0 else nc.vector.tensor_copy
                interleave(
                    grouped[:].rearrange("p (c i) t -> p c t i", i=4),
                    dw_raw[a, h][:, :, c0 : c0 + P].rearrange("p t (c i) -> p c t i", i=4),
                )
                nc.vector.quantize_mx(
                    out=dw_codes[a, n][:].bitcast(FP8X4),
                    scales=dw_scales[a, n][:],
                    in_=grouped[:].rearrange("p c t -> p (c t)"),
                )

        for n in range(N_TILES):
            for a in range(PASSES):
                for g in range(G):
                    nc.tensor.matmul_mx(
                        out=banks[n][:],
                        lhsT=dw_codes[a, n][:].bitcast(FP8X4),
                        lhsT_scale=dw_scales[a, n][:],
                        rhs=bag_words[a][g][:].bitcast(FP8X4),
                        rhs_scale=bag_scales[a][g],
                        start=False,
                        stop=(a == PASSES - 1 and g == G - 1),
                    )
            result = stage.tile([P, S], F32, name="result")
            empty = nc.scalar.copy if n < N_TILES - 1 else nc.vector.tensor_copy
            empty(result[:], banks[n][:])
            nc.sync.dma_start(out[n * P : (n + 1) * P, :], result[:])
